import numpy as np
import ml_dtypes


def mxq(x, axis, fmt="e4m3"):
    dtype, down = {"e4m3": (ml_dtypes.float8_e4m3fn, 7), "e5m2": (ml_dtypes.float8_e5m2, 14)}[fmt]
    v = np.moveaxis(np.asarray(x, np.float32).astype(ml_dtypes.bfloat16).astype(np.float64), axis, -1)
    blocks = v.reshape(v.shape[:-1] + (-1, 32))
    amax = np.abs(blocks).max(-1, keepdims=True)
    byte = np.maximum(np.where(amax > 0, np.frexp(amax)[1] - 1 + 127, 0) - down, 1)
    scale = np.exp2(byte - 127.0)
    codes = (blocks / scale).astype(np.float32).astype(dtype).astype(np.float64)
    return np.moveaxis((codes * scale).reshape(v.shape), -1, axis)


WIDE = False


def mx_kscale(k):
    if not WIDE:
        return np.ones(k)
    levels = np.array([10, -10, 5, -5, 0])
    if k % 512:
        return np.exp2(np.random.permutation(np.resize(levels, k // 32))).repeat(32)
    a = np.empty((k // 512, 16))
    for p in range(k // 512):
        a[p, :8] = np.random.permutation(np.resize(levels, 8))
        for g in range(8):
            far = levels[np.abs(levels - a[p, g]) >= 10]
            a[p, g + 8] = far[np.random.randint(len(far))]
    return np.exp2(a.ravel()).repeat(32)


def f64(x):
    return np.asarray(x).astype(np.float64)


def striped8(idx):
    return np.asarray(idx).reshape(8, -1, 16).transpose(0, 2, 1).reshape(128, -1).astype(np.uint16)


def unstriped8(offs):
    return offs.reshape(8, 16, -1).transpose(0, 2, 1).reshape(8, -1).astype(np.int64)


def pick8(x, idx, run):
    r = np.arange(len(x))
    return x[r[:, None], idx[r % (8 * run) // run]]


E2M1 = np.array([0.0, 0.5, 1.0, 1.5, 2.0, 3.0, 4.0, 6.0, -0.0, -0.5, -1.0, -1.5, -2.0, -3.0, -4.0, -6.0])


def pack_weight(w, fmt):
    k, n = w.shape
    w = f64(np.asarray(w, np.float32).astype(ml_dtypes.bfloat16)).reshape(k // 32, 32, n)
    amax = np.abs(w).max(1)
    if fmt == "e4m3":
        byte = np.frexp(amax)[1] - 1 + 127 - 7
    else:
        mant, ex = np.frexp(amax / 6.0)
        byte = np.where(mant > 0.5, ex, ex - 1) + 127
    byte = np.clip(np.where(amax > 0, byte, 1), 1, 254)
    scaled = (w * np.exp2(127.0 - byte)[:, None, :]).reshape(k, n).astype(np.float32)
    by_word = np.ascontiguousarray(scaled.reshape(k // 512, 128, 4, n).transpose(0, 1, 3, 2))
    if fmt == "e4m3":
        words = by_word.astype(ml_dtypes.float8_e4m3fn).view(np.uint8)
    else:
        c = by_word.astype(ml_dtypes.float4_e2m1fn).view(np.uint8) & 0xF
        words = (c[..., 0::2] | (c[..., 1::2] << 4)).reshape(k // 512, 128, 2 * n)
    return np.ascontiguousarray(words), np.ascontiguousarray(byte.astype(np.uint8).reshape(k // 512, 16, n))


def unpack_weight(words, scales, fmt):
    g, _, n = scales.shape
    words = np.ascontiguousarray(words).reshape(g, 128, n, -1)
    if fmt == "e4m3":
        vals = words.view(ml_dtypes.float8_e4m3fn).astype(np.float64)
    else:
        nib = np.empty((g, 128, n, 4), np.uint8)
        nib[..., 0::2] = words & 0xF
        nib[..., 1::2] = words >> 4
        vals = E2M1[nib]
    vals = vals * np.repeat(np.exp2(scales.astype(np.float64) - 127.0), 8, axis=1)[..., None]
    return vals.transpose(0, 1, 3, 2).reshape(g * 512, n)


D, T, U, I, Q = 512, 1024, 1024, 512, 128


def setup_inputs():
    n = np.random.standard_normal
    idx = np.stack([np.random.permutation(T)[:I] for _ in range(8)])
    idx2 = np.stack([np.random.permutation(U)[:I] for _ in range(8)])
    idx3 = np.stack([np.random.permutation(T)[:I] for _ in range(8)])
    idx4 = np.stack([np.random.permutation(T)[:I] for _ in range(8)])
    idx5 = np.stack([np.random.permutation(U)[:I] for _ in range(8)])
    fd = mx_kscale(D)
    keysp = pack_weight(n((D, T)) / fd[:, None], "e2m1")
    notesp = pack_weight(n((D, U)) / fd[:, None], "e4m3")
    return {
        "query": (n((D, Q)) * 1.0 / np.sqrt(D) * fd[:, None]).astype(np.float32),
        "keys_words": keysp[0],
        "keys_scales": keysp[1],
        "notes_words": notesp[0],
        "notes_scales": notesp[1],
        "offs": striped8(idx),
        "offs2": striped8(idx2),
        "offs3": striped8(idx3),
        "offs4": striped8(idx4),
        "offs5": striped8(idx5),
    }


def reference(query, keys_words, keys_scales, notes_words, notes_scales, offs, offs2, offs3, offs4, offs5):
    idx = unstriped8(offs)
    idx2 = unstriped8(offs2)
    idx3 = unstriped8(offs3)
    idx4 = unstriped8(offs4)
    idx5 = unstriped8(offs5)
    keysu = unpack_weight(keys_words, keys_scales, "e2m1")
    notesu = unpack_weight(notes_words, notes_scales, "e4m3")
    queryq = mxq(f64(query), 0, "e4m3")
    a = queryq.T @ keysu
    b = queryq.T @ notesu
    f1 = np.zeros((Q, U))
    f1[np.arange(Q)[:, None], idx2[np.arange(Q) % 128 // 16]] = pick8(a, idx, 16)
    f2 = np.zeros((Q, T))
    f2[np.arange(Q)[:, None], idx3[np.arange(Q) % 128 // 16]] = pick8(b, idx2, 16)
    bb = b - f1
    aa = a + f2
    v = pick8(aa, idx4, 16) + pick8(bb, idx5, 16)
    y = np.maximum(v, pick8(aa, idx, 16))
    return y

@@ -1,0 +1,154 @@
+from contextlib import ExitStack
+
+import concourse.mybir as mybir
+
+D, T, U, I, Q = 512, 1024, 1024, 512, 128
+FLOPS = 2 * D * Q * (T + U)
+
+F32 = mybir.dt.float32
+BF16 = mybir.dt.bfloat16
+I32 = mybir.dt.int32
+U32 = mybir.dt.uint32
+U16 = mybir.dt.uint16
+U8 = mybir.dt.uint8
+FP8X4 = mybir.dt.float8_e4m3fn_x4
+FP4X4 = mybir.dt.float4_e2m1fn_x4
+ADD = mybir.AluOpType.add
+SUB = mybir.AluOpType.subtract
+MAX = mybir.AluOpType.max
+COPY = mybir.ActivationFunctionType.Copy
+
+P = 128
+PACK = 4
+GROUP = 16
+HALF = I // 2
+NOTE_COLS = 256
+KEY_COLS = 512
+
+
+def load_scales(nc, plane, scales):
+    for r in range(4):
+        nc.sync.dma_start(plane[r:P:32, :].bitcast(I32), scales[0, r:16:4, :].bitcast(I32))
+
+
+def entries(lists, first, last):
+    return lists[:, first // GROUP : last // GROUP]
+
+
+def tile_attend_postboxes_two_kernel(
+    tc, query, keys_words, keys_scales, notes_words, notes_scales, offs, offs2, offs3, offs4, offs5, out
+):
+    nc = tc.nc
+    with ExitStack() as ctx:
+        held = ctx.enter_context(tc.tile_pool(name="held", bufs=1))
+        psum = ctx.enter_context(tc.psum_pool(name="psum", bufs=1))
+
+        idx = held.tile([P, I // GROUP], U16)
+        idx2 = held.tile([P, I // GROUP], U16)
+        idx3 = held.tile([P, I // GROUP], U16)
+        idx4 = held.tile([P, I // GROUP], U16)
+        idx5 = held.tile([P, I // GROUP], U16)
+
+        q_raw = held.tile([P, PACK, Q], F32)
+        q_bf = held.tile([P, Q, PACK], BF16, align_bytes=64)
+        q_codes = held.tile([P, Q], U32, align_bytes=64)
+        q_plane = held.tile([P, Q], U8, align_bytes=64)
+        note_codes = held.tile([P, U], U32, align_bytes=64)
+        note_plane = held.tile([P, U], U8, align_bytes=64)
+        key_codes = held.tile([P, 2 * T], U8, align_bytes=64)
+        key_plane = held.tile([P, T], U8, align_bytes=64)
+
+        a = held.tile([P, T], F32)
+        b = held.tile([P, U], F32)
+        f1 = held.tile([P, U], F32)
+        f2 = held.tile([P, T], F32)
+        aa = held.tile([P, T], F32)
+        bb = held.tile([P, U], F32)
+        a_idx = held.tile([P, I], F32)
+        b_idx2 = held.tile([P, I], F32)
+        aa_idx4 = held.tile([P, I], F32)
+        aa_idx = held.tile([P, I], F32)
+        bb_idx5 = held.tile([P, HALF], F32)
+        v = held.tile([P, I], F32)
+        y = held.tile([P, I], F32)
+
+        nc.vector.memset(note_plane[:].bitcast(U32), 0)
+        nc.vector.memset(key_plane[:].bitcast(U32), 0)
+        nc.vector.memset(f2[:], 0.0)
+        nc.vector.memset(f1[:], 0.0)
+
+        nc.sync.dma_start(q_raw[:], query.rearrange("(p j) q -> p j q", j=PACK))
+        load_scales(nc, note_plane, notes_scales)
+        note_words = notes_words[0].rearrange("p n t -> p (n t)").bitcast(I32)
+        for cols in (slice(0, U // 2), slice(U // 2, U)):
+            nc.sync.dma_start(note_codes[:, cols].bitcast(I32), note_words[:, cols])
+        nc.sync.dma_start(idx2[:], offs2)
+        nc.sync.dma_start(idx3[:], offs3)
+        nc.sync.dma_start(key_codes[:].bitcast(I32), keys_words[0].bitcast(I32))
+        load_scales(nc, key_plane, keys_scales)
+        nc.sync.dma_start(idx[:], offs)
+        nc.sync.dma_start(idx4[:], offs4)
+        nc.sync.dma_start(idx5[:], offs5)
+
+        q_halves = [slice(0, Q // 2), slice(Q // 2, Q)]
+        for rows in q_halves:
+            nc.vector.tensor_copy(
+                q_bf[:, rows, :].rearrange("p (c i) j -> p c j i", i=4),
+                q_raw[:, :, rows].rearrange("p j (c i) -> p c j i", i=4),
+            )
+        for rows in q_halves:
+            nc.vector.quantize_mx(
+                out=q_codes[:, rows].bitcast(FP8X4),
+                scales=q_plane[:, rows],
+                in_=q_bf[:, rows, :].rearrange("p q j -> p (q j)"),
+            )
+
+        for n in range(U // NOTE_COLS):
+            cols = slice(n * NOTE_COLS, (n + 1) * NOTE_COLS)
+            bank = psum.tile([P, NOTE_COLS], F32, tag=f"bank{n}", name=f"b_bank{n}")[:]
+            nc.tensor.matmul_mx(
+                out=bank,
+                lhsT=q_codes[:].bitcast(FP8X4),
+                lhsT_scale=q_plane[:],
+                rhs=note_codes[:, cols].bitcast(FP8X4),
+                rhs_scale=note_plane[:, cols],
+                start=True,
+                stop=True,
+            )
+            if n % 2 == 0:
+                nc.scalar.copy(b[:, cols], bank)
+            else:
+                nc.vector.tensor_copy(b[:, cols], bank)
+
+        nc.vector.tensor_copy(b_idx2[:, :HALF], b[:].indirect(entries(idx2, 0, HALF)))
+        nc.scalar.activation(b_idx2[:, HALF:], b[:].indirect(entries(idx2, HALF, I)), COPY)
+        nc.vector.tensor_copy(f2[:].indirect(idx3[:]), b_idx2[:])
+
+        for n in range(T // KEY_COLS):
+            cols = slice(n * KEY_COLS, (n + 1) * KEY_COLS)
+            bank = psum.tile([P, KEY_COLS], F32, tag=f"bank{2 + n}", name=f"a_bank{n}")[:]
+            nc.tensor.matmul_mx(
+                out=bank,
+                lhsT=q_codes[:].bitcast(FP8X4),
+                lhsT_scale=q_plane[:],
+                rhs=key_codes[:, 2 * n * KEY_COLS : 2 * (n + 1) * KEY_COLS].bitcast(FP4X4),
+                rhs_scale=key_plane[:, cols],
+                start=True,
+                stop=True,
+            )
+            nc.scalar.copy(a[:, cols], bank)
+
+        nc.scalar.activation(a_idx[:], a[:].indirect(idx[:]), COPY)
+        nc.vector.tensor_tensor(aa[:], a[:], f2[:], ADD)
+        nc.vector.tensor_copy(f1[:].indirect(idx2[:]), a_idx[:])
+        nc.scalar.activation(aa_idx4[:], aa[:].indirect(idx4[:]), COPY)
+        nc.scalar.activation(aa_idx[:], aa[:].indirect(idx[:]), COPY)
+        nc.vector.tensor_tensor(bb[:], b[:], f1[:], SUB)
+
+        nc.vector.tensor_tensor(v[:, :HALF], bb[:].indirect(entries(idx5, 0, HALF)), aa_idx4[:, :HALF], ADD)
+        nc.scalar.activation(bb_idx5[:], bb[:].indirect(entries(idx5, HALF, I)), COPY)
+        nc.vector.tensor_tensor(v[:, HALF:], bb_idx5[:], aa_idx4[:, HALF:], ADD)
+        nc.vector.tensor_tensor(y[:, :HALF], v[:, :HALF], aa_idx[:, :HALF], MAX)
+        nc.sync.dma_start(out[:, :HALF], y[:, :HALF])
+        nc.vector.tensor_tensor(y[:, HALF:], v[:, HALF:], aa_idx[:, HALF:], MAX)
+        nc.sync.dma_start(out[:, HALF:], y[:, HALF:])

@@ -58,19 +58,18 @@ def tile_attend_postboxes_two_kernel(
         key_codes = held.tile([P, 2 * T], U8, align_bytes=64)
         key_plane = held.tile([P, T], U8, align_bytes=64)
 
-        a = held.tile([P, T], F32)
-        b = held.tile([P, U], F32)
+        a = held.tile([P, T], F32, tag="a")
+        b = held.tile([P, U], F32, tag="b")
         f1 = held.tile([P, U], F32)
         f2 = held.tile([P, T], F32)
         aa = held.tile([P, T], F32)
-        bb = held.tile([P, U], F32)
         a_idx = held.tile([P, I], F32)
         b_idx2 = held.tile([P, I], F32)
         aa_idx4 = held.tile([P, I], F32)
-        aa_idx = held.tile([P, I], F32)
+        aa_idx_lo = held.tile([P, HALF], F32)
         bb_idx5 = held.tile([P, HALF], F32)
         v = held.tile([P, I], F32)
-        y = held.tile([P, I], F32)
+        y_hi = held.tile([P, HALF], F32)
 
         nc.vector.memset(note_plane[:].bitcast(U32), 0)
         nc.vector.memset(key_plane[:].bitcast(U32), 0)
@@ -139,16 +138,21 @@ def tile_attend_postboxes_two_kernel(
             nc.scalar.copy(a[:, cols], bank)
 
         nc.scalar.activation(a_idx[:], a[:].indirect(idx[:]), COPY)
-        nc.vector.tensor_tensor(aa[:], a[:], f2[:], ADD)
+        nc.gpsimd.tensor_tensor(aa[:], a[:], f2[:], ADD)
         nc.vector.tensor_copy(f1[:].indirect(idx2[:]), a_idx[:])
-        nc.scalar.activation(aa_idx4[:], aa[:].indirect(idx4[:]), COPY)
-        nc.scalar.activation(aa_idx[:], aa[:].indirect(idx[:]), COPY)
+        nc.scalar.activation(aa_idx4[:, :HALF], aa[:].indirect(entries(idx4, 0, HALF)), COPY)
+        nc.scalar.activation(aa_idx4[:, HALF:], aa[:].indirect(entries(idx4, HALF, I)), COPY)
+        nc.scalar.activation(aa_idx_lo[:], aa[:].indirect(entries(idx, 0, HALF)), COPY)
+        bb = held.tile([P, U], F32, tag="a")
         nc.vector.tensor_tensor(bb[:], b[:], f1[:], SUB)
 
         nc.vector.tensor_tensor(v[:, :HALF], bb[:].indirect(entries(idx5, 0, HALF)), aa_idx4[:, :HALF], ADD)
         nc.scalar.activation(bb_idx5[:], bb[:].indirect(entries(idx5, HALF, I)), COPY)
+        aa_idx_hi = held.tile([P, HALF], F32, tag="b")
+        nc.scalar.activation(aa_idx_hi[:], aa[:].indirect(entries(idx, HALF, I)), COPY)
         nc.vector.tensor_tensor(v[:, HALF:], bb_idx5[:], aa_idx4[:, HALF:], ADD)
-        nc.vector.tensor_tensor(y[:, :HALF], v[:, :HALF], aa_idx[:, :HALF], MAX)
-        nc.sync.dma_start(out[:, :HALF], y[:, :HALF])
-        nc.vector.tensor_tensor(y[:, HALF:], v[:, HALF:], aa_idx[:, HALF:], MAX)
-        nc.sync.dma_start(out[:, HALF:], y[:, HALF:])
+        y_lo = held.tile([P, HALF], F32, tag="a")
+        nc.vector.tensor_tensor(y_lo[:], v[:, :HALF], aa_idx_lo[:], MAX)
+        nc.sync.dma_start(out[:, :HALF], y_lo[:])
+        nc.vector.tensor_tensor(y_hi[:], v[:, HALF:], aa_idx_hi[:], MAX)
+        nc.sync.dma_start(out[:, HALF:], y_hi[:])

@@ -22,8 +22,9 @@ P = 128
 PACK = 4
 GROUP = 16
 HALF = I // 2
-NOTE_COLS = 256
-KEY_COLS = 512
+KEY_PIECES = (256, 256, 256, 128, 128)
+NOTE_COLS = 512
+KEPT = 3
 
 
 def load_scales(nc, plane, scales):
@@ -58,55 +59,77 @@ def tile_attend_postboxes_two_kernel(
         key_codes = held.tile([P, 2 * T], U8, align_bytes=64)
         key_plane = held.tile([P, T], U8, align_bytes=64)
 
-        a = held.tile([P, T], F32, tag="a")
-        b = held.tile([P, U], F32, tag="b")
+        a = held.tile([P, T], F32)
+        b = held.tile([P, U], F32)
         f1 = held.tile([P, U], F32)
         f2 = held.tile([P, T], F32)
         aa = held.tile([P, T], F32)
+        bb = held.tile([P, U], F32)
         a_idx = held.tile([P, I], F32)
         b_idx2 = held.tile([P, I], F32)
-        aa_idx4 = held.tile([P, I], F32)
-        aa_idx_lo = held.tile([P, HALF], F32)
-        bb_idx5 = held.tile([P, HALF], F32)
+        bb_idx5 = held.tile([P, I], F32)
+        aa_idx = held.tile([P, I], F32)
         v = held.tile([P, I], F32)
-        y_hi = held.tile([P, HALF], F32)
+        y = held.tile([P, I], F32)
 
-        nc.vector.memset(note_plane[:].bitcast(U32), 0)
         nc.vector.memset(key_plane[:].bitcast(U32), 0)
-        nc.vector.memset(f2[:], 0.0)
+        nc.vector.memset(note_plane[:].bitcast(U32), 0)
         nc.vector.memset(f1[:], 0.0)
+        nc.vector.memset(f2[:], 0.0)
 
         nc.sync.dma_start(q_raw[:], query.rearrange("(p j) q -> p j q", j=PACK))
-        load_scales(nc, note_plane, notes_scales)
-        note_words = notes_words[0].rearrange("p n t -> p (n t)").bitcast(I32)
-        for cols in (slice(0, U // 2), slice(U // 2, U)):
-            nc.sync.dma_start(note_codes[:, cols].bitcast(I32), note_words[:, cols])
-        nc.sync.dma_start(idx2[:], offs2)
-        nc.sync.dma_start(idx3[:], offs3)
-        nc.sync.dma_start(key_codes[:].bitcast(I32), keys_words[0].bitcast(I32))
         load_scales(nc, key_plane, keys_scales)
+        nc.sync.dma_start(key_codes[:].bitcast(I32), keys_words[0].bitcast(I32))
         nc.sync.dma_start(idx[:], offs)
-        nc.sync.dma_start(idx4[:], offs4)
+        nc.sync.dma_start(idx2[:], offs2)
+        nc.sync.dma_start(note_codes[:].bitcast(I32), notes_words[0].rearrange("p n t -> p (n t)").bitcast(I32))
+        load_scales(nc, note_plane, notes_scales)
+        nc.sync.dma_start(idx3[:], offs3)
         nc.sync.dma_start(idx5[:], offs5)
+        nc.sync.dma_start(idx4[:], offs4)
 
-        q_halves = [slice(0, Q // 2), slice(Q // 2, Q)]
-        for rows in q_halves:
-            nc.vector.tensor_copy(
-                q_bf[:, rows, :].rearrange("p (c i) j -> p c j i", i=4),
-                q_raw[:, :, rows].rearrange("p j (c i) -> p c j i", i=4),
+        nc.vector.tensor_copy(
+            q_bf[:, : Q // 2, :].rearrange("p (c i) j -> p c j i", i=4),
+            q_raw[:, :, : Q // 2].rearrange("p j (c i) -> p c j i", i=4),
+        )
+        nc.scalar.copy(
+            q_bf[:, Q // 2 :, :].rearrange("p (c i) j -> p c j i", i=4),
+            q_raw[:, :, Q // 2 :].rearrange("p j (c i) -> p c j i", i=4),
+        )
+        nc.vector.quantize_mx(
+            out=q_codes[:].bitcast(FP8X4), scales=q_plane[:], in_=q_bf[:].rearrange("p q j -> p (q j)")
+        )
+
+        a_banks = []
+        first = 0
+        for n, width in enumerate(KEY_PIECES):
+            cols = slice(first, first + width)
+            bank = psum.tile([P, width], F32, tag=f"bank{n}", name=f"a_bank{n}")
+            nc.tensor.matmul_mx(
+                out=bank[:],
+                lhsT=q_codes[:].bitcast(FP8X4),
+                lhsT_scale=q_plane[:],
+                rhs=key_codes[:, 2 * first : 2 * (first + width)].bitcast(FP4X4),
+                rhs_scale=key_plane[:, cols],
+                start=True,
+                stop=True,
             )
-        for rows in q_halves:
-            nc.vector.quantize_mx(
-                out=q_codes[:, rows].bitcast(FP8X4),
-                scales=q_plane[:, rows],
-                in_=q_bf[:, rows, :].rearrange("p q j -> p (q j)"),
-            )
+            if n % 2 == 0:
+                nc.scalar.copy(a[:, cols], bank[:])
+            else:
+                nc.vector.tensor_copy(a[:, cols], bank[:])
+            a_banks.append((cols, bank))
+            first += width
+
+        nc.vector.tensor_copy(a_idx[:, :HALF], a[:].indirect(entries(idx, 0, HALF)))
+        nc.scalar.activation(a_idx[:, HALF:], a[:].indirect(entries(idx, HALF, I)), COPY)
+        nc.vector.tensor_copy(f1[:].indirect(idx2[:]), a_idx[:])
 
         for n in range(U // NOTE_COLS):
             cols = slice(n * NOTE_COLS, (n + 1) * NOTE_COLS)
-            bank = psum.tile([P, NOTE_COLS], F32, tag=f"bank{n}", name=f"b_bank{n}")[:]
+            bank = psum.tile([P, NOTE_COLS], F32, tag=f"bank{KEPT + n}", name=f"b_bank{n}")
             nc.tensor.matmul_mx(
-                out=bank,
+                out=bank[:],
                 lhsT=q_codes[:].bitcast(FP8X4),
                 lhsT_scale=q_plane[:],
                 rhs=note_codes[:, cols].bitcast(FP8X4),
@@ -114,45 +137,20 @@ def tile_attend_postboxes_two_kernel(
                 start=True,
                 stop=True,
             )
-            if n % 2 == 0:
-                nc.scalar.copy(b[:, cols], bank)
-            else:
-                nc.vector.tensor_copy(b[:, cols], bank)
+            nc.scalar.copy(b[:, cols], bank[:])
 
-        nc.vector.tensor_copy(b_idx2[:, :HALF], b[:].indirect(entries(idx2, 0, HALF)))
-        nc.scalar.activation(b_idx2[:, HALF:], b[:].indirect(entries(idx2, HALF, I)), COPY)
+        nc.scalar.activation(b_idx2[:], b[:].indirect(idx2[:]), COPY)
+        nc.gpsimd.tensor_tensor(bb[:], b[:], f1[:], SUB)
         nc.vector.tensor_copy(f2[:].indirect(idx3[:]), b_idx2[:])
+        nc.scalar.activation(bb_idx5[:], bb[:].indirect(idx5[:]), COPY)
+        for cols, bank in a_banks[:KEPT]:
+            nc.vector.tensor_tensor(aa[:, cols], bank[:], f2[:, cols], ADD)
+        rest = slice(sum(KEY_PIECES[:KEPT]), T)
+        nc.gpsimd.tensor_tensor(aa[:, rest], a[:, rest], f2[:, rest], ADD)
 
-        for n in range(T // KEY_COLS):
-            cols = slice(n * KEY_COLS, (n + 1) * KEY_COLS)
-            bank = psum.tile([P, KEY_COLS], F32, tag=f"bank{2 + n}", name=f"a_bank{n}")[:]
-            nc.tensor.matmul_mx(
-                out=bank,
-                lhsT=q_codes[:].bitcast(FP8X4),
-                lhsT_scale=q_plane[:],
-                rhs=key_codes[:, 2 * n * KEY_COLS : 2 * (n + 1) * KEY_COLS].bitcast(FP4X4),
-                rhs_scale=key_plane[:, cols],
-                start=True,
-                stop=True,
-            )
-            nc.scalar.copy(a[:, cols], bank)
-
-        nc.scalar.activation(a_idx[:], a[:].indirect(idx[:]), COPY)
-        nc.gpsimd.tensor_tensor(aa[:], a[:], f2[:], ADD)
-        nc.vector.tensor_copy(f1[:].indirect(idx2[:]), a_idx[:])
-        nc.scalar.activation(aa_idx4[:, :HALF], aa[:].indirect(entries(idx4, 0, HALF)), COPY)
-        nc.scalar.activation(aa_idx4[:, HALF:], aa[:].indirect(entries(idx4, HALF, I)), COPY)
-        nc.scalar.activation(aa_idx_lo[:], aa[:].indirect(entries(idx, 0, HALF)), COPY)
-        bb = held.tile([P, U], F32, tag="a")
-        nc.vector.tensor_tensor(bb[:], b[:], f1[:], SUB)
-
-        nc.vector.tensor_tensor(v[:, :HALF], bb[:].indirect(entries(idx5, 0, HALF)), aa_idx4[:, :HALF], ADD)
-        nc.scalar.activation(bb_idx5[:], bb[:].indirect(entries(idx5, HALF, I)), COPY)
-        aa_idx_hi = held.tile([P, HALF], F32, tag="b")
-        nc.scalar.activation(aa_idx_hi[:], aa[:].indirect(entries(idx, HALF, I)), COPY)
-        nc.vector.tensor_tensor(v[:, HALF:], bb_idx5[:], aa_idx4[:, HALF:], ADD)
-        y_lo = held.tile([P, HALF], F32, tag="a")
-        nc.vector.tensor_tensor(y_lo[:], v[:, :HALF], aa_idx_lo[:], MAX)
-        nc.sync.dma_start(out[:, :HALF], y_lo[:])
-        nc.vector.tensor_tensor(y_hi[:], v[:, HALF:], aa_idx_hi[:], MAX)
-        nc.sync.dma_start(out[:, HALF:], y_hi[:])
+        for lo, hi in ((0, HALF), (HALF, I)):
+            nc.vector.tensor_tensor(v[:, lo:hi], aa[:].indirect(entries(idx4, lo, hi)), bb_idx5[:, lo:hi], ADD)
+            nc.scalar.activation(aa_idx[:, lo:hi], aa[:].indirect(entries(idx, lo, hi)), COPY)
+        for lo, hi in ((0, HALF), (HALF, I)):
+            nc.vector.tensor_tensor(y[:, lo:hi], v[:, lo:hi], aa_idx[:, lo:hi], MAX)
+            nc.sync.dma_start(out[:, lo:hi], y[:, lo:hi])

@@ -78,8 +78,8 @@ def tile_attend_postboxes_two_kernel(
         nc.vector.memset(f2[:], 0.0)
 
         nc.sync.dma_start(q_raw[:], query.rearrange("(p j) q -> p j q", j=PACK))
-        load_scales(nc, key_plane, keys_scales)
         nc.sync.dma_start(key_codes[:].bitcast(I32), keys_words[0].bitcast(I32))
+        load_scales(nc, key_plane, keys_scales)
         nc.sync.dma_start(idx[:], offs)
         nc.sync.dma_start(idx2[:], offs2)
         nc.sync.dma_start(note_codes[:].bitcast(I32), notes_words[0].rearrange("p n t -> p (n t)").bitcast(I32))
@@ -89,12 +89,12 @@ def tile_attend_postboxes_two_kernel(
         nc.sync.dma_start(idx4[:], offs4)
 
         nc.vector.tensor_copy(
-            q_bf[:, : Q // 2, :].rearrange("p (c i) j -> p c j i", i=4),
-            q_raw[:, :, : Q // 2].rearrange("p j (c i) -> p c j i", i=4),
+            q_bf[:, : 72, :].rearrange("p (c i) j -> p c j i", i=4),
+            q_raw[:, :, : 72].rearrange("p j (c i) -> p c j i", i=4),
         )
         nc.scalar.copy(
-            q_bf[:, Q // 2 :, :].rearrange("p (c i) j -> p c j i", i=4),
-            q_raw[:, :, Q // 2 :].rearrange("p j (c i) -> p c j i", i=4),
+            q_bf[:, 72 :, :].rearrange("p (c i) j -> p c j i", i=4),
+            q_raw[:, :, 72 :].rearrange("p j (c i) -> p c j i", i=4),
         )
         nc.vector.quantize_mx(
             out=q_codes[:].bitcast(FP8X4), scales=q_plane[:], in_=q_bf[:].rearrange("p q j -> p (q j)")
@@ -144,9 +144,9 @@ def tile_attend_postboxes_two_kernel(
         nc.vector.tensor_copy(f2[:].indirect(idx3[:]), b_idx2[:])
         nc.scalar.activation(bb_idx5[:], bb[:].indirect(idx5[:]), COPY)
         for cols, bank in a_banks[:KEPT]:
-            nc.vector.tensor_tensor(aa[:, cols], bank[:], f2[:, cols], ADD)
-        rest = slice(sum(KEY_PIECES[:KEPT]), T)
-        nc.gpsimd.tensor_tensor(aa[:, rest], a[:, rest], f2[:, rest], ADD)
+            stop = min(cols.stop, 704)
+            nc.vector.tensor_tensor(aa[:, cols.start : stop], bank[:, : stop - cols.start], f2[:, cols.start : stop], ADD)
+        nc.gpsimd.tensor_tensor(aa[:, 704:], a[:, 704:], f2[:, 704:], ADD)
 
         for lo, hi in ((0, HALF), (HALF, I)):
             nc.vector.tensor_tensor(v[:, lo:hi], aa[:].indirect(entries(idx4, lo, hi)), bb_idx5[:, lo:hi], ADD)

from contextlib import ExitStack

import concourse.mybir as mybir

D, T, U, I, Q = 512, 1024, 1024, 512, 128
FLOPS = 2 * D * Q * (T + U)

F32 = mybir.dt.float32
BF16 = mybir.dt.bfloat16
I32 = mybir.dt.int32
U32 = mybir.dt.uint32
U16 = mybir.dt.uint16
U8 = mybir.dt.uint8
FP8X4 = mybir.dt.float8_e4m3fn_x4
FP4X4 = mybir.dt.float4_e2m1fn_x4
ADD = mybir.AluOpType.add
SUB = mybir.AluOpType.subtract
MAX = mybir.AluOpType.max
COPY = mybir.ActivationFunctionType.Copy

P = 128
PACK = 4
GROUP = 16
HALF = I // 2
KEY_PIECES = (256, 256, 256, 128, 128)
NOTE_COLS = 512
KEPT = 3


def load_scales(nc, plane, scales):
    for r in range(4):
        nc.sync.dma_start(plane[r:P:32, :].bitcast(I32), scales[0, r:16:4, :].bitcast(I32))


def entries(lists, first, last):
    return lists[:, first // GROUP : last // GROUP]


def tile_attend_postboxes_two_kernel(
    tc, query, keys_words, keys_scales, notes_words, notes_scales, offs, offs2, offs3, offs4, offs5, out
):
    nc = tc.nc
    with ExitStack() as ctx:
        held = ctx.enter_context(tc.tile_pool(name="held", bufs=1))
        psum = ctx.enter_context(tc.psum_pool(name="psum", bufs=1))

        idx = held.tile([P, I // GROUP], U16)
        idx2 = held.tile([P, I // GROUP], U16)
        idx3 = held.tile([P, I // GROUP], U16)
        idx4 = held.tile([P, I // GROUP], U16)
        idx5 = held.tile([P, I // GROUP], U16)

        q_raw = held.tile([P, PACK, Q], F32)
        q_bf = held.tile([P, Q, PACK], BF16, align_bytes=64)
        q_codes = held.tile([P, Q], U32, align_bytes=64)
        q_plane = held.tile([P, Q], U8, align_bytes=64)
        note_codes = held.tile([P, U], U32, align_bytes=64)
        note_plane = held.tile([P, U], U8, align_bytes=64)
        key_codes = held.tile([P, 2 * T], U8, align_bytes=64)
        key_plane = held.tile([P, T], U8, align_bytes=64)

        a = held.tile([P, T], F32)
        b = held.tile([P, U], F32)
        f1 = held.tile([P, U], F32)
        f2 = held.tile([P, T], F32)
        aa = held.tile([P, T], F32)
        bb = held.tile([P, U], F32)
        a_idx = held.tile([P, I], F32)
        b_idx2 = held.tile([P, I], F32)
        bb_idx5 = held.tile([P, I], F32)
        aa_idx = held.tile([P, I], F32)
        v = held.tile([P, I], F32)
        y = held.tile([P, I], F32)

        nc.vector.memset(key_plane[:].bitcast(U32), 0)
        nc.vector.memset(note_plane[:].bitcast(U32), 0)
        nc.vector.memset(f1[:], 0.0)
        nc.vector.memset(f2[:], 0.0)

        nc.sync.dma_start(q_raw[:], query.rearrange("(p j) q -> p j q", j=PACK))
        nc.sync.dma_start(key_codes[:].bitcast(I32), keys_words[0].bitcast(I32))
        load_scales(nc, key_plane, keys_scales)
        nc.sync.dma_start(idx[:], offs)
        nc.sync.dma_start(idx2[:], offs2)
        nc.sync.dma_start(note_codes[:].bitcast(I32), notes_words[0].rearrange("p n t -> p (n t)").bitcast(I32))
        load_scales(nc, note_plane, notes_scales)
        nc.sync.dma_start(idx3[:], offs3)
        nc.sync.dma_start(idx5[:], offs5)
        nc.sync.dma_start(idx4[:], offs4)

        nc.vector.tensor_copy(
            q_bf[:, : 72, :].rearrange("p (c i) j -> p c j i", i=4),
            q_raw[:, :, : 72].rearrange("p j (c i) -> p c j i", i=4),
        )
        nc.scalar.copy(
            q_bf[:, 72 :, :].rearrange("p (c i) j -> p c j i", i=4),
            q_raw[:, :, 72 :].rearrange("p j (c i) -> p c j i", i=4),
        )
        nc.vector.quantize_mx(
            out=q_codes[:].bitcast(FP8X4), scales=q_plane[:], in_=q_bf[:].rearrange("p q j -> p (q j)")
        )

        a_banks = []
        first = 0
        for n, width in enumerate(KEY_PIECES):
            cols = slice(first, first + width)
            bank = psum.tile([P, width], F32, tag=f"bank{n}", name=f"a_bank{n}")
            nc.tensor.matmul_mx(
                out=bank[:],
                lhsT=q_codes[:].bitcast(FP8X4),
                lhsT_scale=q_plane[:],
                rhs=key_codes[:, 2 * first : 2 * (first + width)].bitcast(FP4X4),
                rhs_scale=key_plane[:, cols],
                start=True,
                stop=True,
            )
            if n % 2 == 0:
                nc.scalar.copy(a[:, cols], bank[:])
            else:
                nc.vector.tensor_copy(a[:, cols], bank[:])
            a_banks.append((cols, bank))
            first += width

        nc.vector.tensor_copy(a_idx[:, :HALF], a[:].indirect(entries(idx, 0, HALF)))
        nc.scalar.activation(a_idx[:, HALF:], a[:].indirect(entries(idx, HALF, I)), COPY)
        nc.vector.tensor_copy(f1[:].indirect(idx2[:]), a_idx[:])

        for n in range(U // NOTE_COLS):
            cols = slice(n * NOTE_COLS, (n + 1) * NOTE_COLS)
            bank = psum.tile([P, NOTE_COLS], F32, tag=f"bank{KEPT + n}", name=f"b_bank{n}")
            nc.tensor.matmul_mx(
                out=bank[:],
                lhsT=q_codes[:].bitcast(FP8X4),
                lhsT_scale=q_plane[:],
                rhs=note_codes[:, cols].bitcast(FP8X4),
                rhs_scale=note_plane[:, cols],
                start=True,
                stop=True,
            )
            nc.scalar.copy(b[:, cols], bank[:])

        nc.scalar.activation(b_idx2[:], b[:].indirect(idx2[:]), COPY)
        nc.gpsimd.tensor_tensor(bb[:], b[:], f1[:], SUB)
        nc.vector.tensor_copy(f2[:].indirect(idx3[:]), b_idx2[:])
        nc.scalar.activation(bb_idx5[:], bb[:].indirect(idx5[:]), COPY)
        for cols, bank in a_banks[:KEPT]:
            stop = min(cols.stop, 704)
            nc.vector.tensor_tensor(aa[:, cols.start : stop], bank[:, : stop - cols.start], f2[:, cols.start : stop], ADD)
        nc.gpsimd.tensor_tensor(aa[:, 704:], a[:, 704:], f2[:, 704:], ADD)

        for lo, hi in ((0, HALF), (HALF, I)):
            nc.vector.tensor_tensor(v[:, lo:hi], aa[:].indirect(entries(idx4, lo, hi)), bb_idx5[:, lo:hi], ADD)
            nc.scalar.activation(aa_idx[:, lo:hi], aa[:].indirect(entries(idx, lo, hi)), COPY)
        for lo, hi in ((0, HALF), (HALF, I)):
            nc.vector.tensor_tensor(y[:, lo:hi], v[:, lo:hi], aa_idx[:, lo:hi], MAX)
            nc.sync.dma_start(out[:, lo:hi], y[:, lo:hi])
